import numpy as np
CORES = [4,5,6,7,12,13,14,15,20,21,22,23,28,29,30,31,36,37,38,39,44,45,46,47]
N = 24
def setup_inputs(rng):
    return {"x": rng.standard_normal((N, 128, 64), dtype=np.float32)}
def reference(x):
    g = np.concatenate(list(x), axis=1)
    return {"y": np.broadcast_to(g, (N,) + g.shape)}

@@ -1,0 +1,73 @@
+import concourse.bass as bass
+
+SCRATCH = {
+    "G": ("sbuf", [128, 1536], "float32"),
+}
+SEMAPHORES = ["ld", "st", "sent", "c0", "c1", "c2", "c3", "c4", "c5"]
+
+
+def rank_program(g, core, T, topo):
+    c, k = divmod(core, 8)
+    G = T.G
+    csem = [T.sem.c0, T.sem.c1, T.sem.c2, T.sem.c3, T.sem.c4, T.sem.c5]
+    m, p1, p2 = c ^ 1, (c + 2) % 6, (c + 4) % 6
+    q1, q2 = p1 ^ 1, p2 ^ 1
+    sent = [0]
+
+    def send(lo, hi, dsts, s):
+        off = any(topo.chip(d) != c for d in dsts)
+        mask, n = (0x00FF, 8) if off else (0xFFFF, 16)
+        ap = G[:, lo:hi]
+        ids = [bass.DstId(rid=topo.addr(d)[0], pnc=topo.addr(d)[1]) for d in dsts]
+        g.remote_dma_fused(
+            [bass.RemoteDMATransfer(dst_ids=ids, dma_engine_mask=mask, remote_sem=csem[s],
+                                    srcs=[ap], dsts=[ap] * len(dsts))],
+            local_sem=T.sem.sent)
+        sent[0] += n
+
+    ranks = [8 * c + j for j in (4, 5, 6, 7)]
+    b0 = 256 * c
+
+    if k >= 4:
+        r = T.rank_of(core)
+        g.dma_start(G[:, 64 * r:64 * r + 64], T.x[:, :]).then_inc(T.sem.ld, 16)
+        g.wait_ge(T.sem.ld, 16)
+        helpers = [8 * c + 0, 8 * c + 2] + ([8 * c + 3] if k >= 6 else [])
+        send(64 * r, 64 * r + 64, [d for d in ranks if d != core] + helpers, c)
+        g.wait_ge(csem[c], 48)
+        if k == 4:
+            send(b0, b0 + 256, [8 * p1 + 1], c)
+        elif k == 6:
+            send(b0, b0 + 256, [8 * q1 + 0], c)
+        elif k == 7:
+            send(b0, b0 + 128, [8 * m + 1], c)
+        nst = 0
+        for s in (c, m, p2, p1, q2, q1):
+            if s == m:
+                g.wait_ge(csem[s], 32)
+            elif s != c:
+                g.wait_ge(csem[s], 16)
+            g.dma_start(T.y[:, 256 * s:256 * s + 256], G[:, 256 * s:256 * s + 256]).then_inc(T.sem.st, 16)
+            nst += 16
+        g.wait_ge(T.sem.st, nst)
+        g.wait_ge(T.sem.sent, sent[0])
+        return
+
+    if k == 0:
+        g.wait_ge(csem[c], 64)
+        send(b0, b0 + 256, [8 * p2 + 3], c)
+        src = [(q2, 0, 256)]
+    elif k == 2:
+        g.wait_ge(csem[c], 64)
+        send(b0, b0 + 256, [8 * q2 + 2], c)
+        src = [(q1, 0, 256)]
+    elif k == 3:
+        g.wait_ge(csem[c], 32)
+        send(b0 + 128, b0 + 256, [8 * m + 3], c)
+        src = [(m, 128, 256), (p1, 0, 256)]
+    else:
+        src = [(m, 0, 128), (p2, 0, 256)]
+    for s, lo, hi in src:
+        g.wait_ge(csem[s], 8)
+        send(256 * s + lo, 256 * s + hi, ranks, s)
+    g.wait_ge(T.sem.sent, sent[0])

@@ -3,7 +3,7 @@ import concourse.bass as bass
 SCRATCH = {
     "G": ("sbuf", [128, 1536], "float32"),
 }
-SEMAPHORES = ["ld", "st", "sent", "c0", "c1", "c2", "c3", "c4", "c5"]
+SEMAPHORES = ["ld", "st", "sent", "ml", "c0", "c1", "c2", "c3", "c4", "c5"]
 
 
 def rank_program(g, core, T, topo):
@@ -14,60 +14,71 @@ def rank_program(g, core, T, topo):
     q1, q2 = p1 ^ 1, p2 ^ 1
     sent = [0]
 
-    def send(lo, hi, dsts, s):
+    def send(lo, hi, dsts, sem):
         off = any(topo.chip(d) != c for d in dsts)
         mask, n = (0x00FF, 8) if off else (0xFFFF, 16)
         ap = G[:, lo:hi]
         ids = [bass.DstId(rid=topo.addr(d)[0], pnc=topo.addr(d)[1]) for d in dsts]
         g.remote_dma_fused(
-            [bass.RemoteDMATransfer(dst_ids=ids, dma_engine_mask=mask, remote_sem=csem[s],
+            [bass.RemoteDMATransfer(dst_ids=ids, dma_engine_mask=mask, remote_sem=sem,
                                     srcs=[ap], dsts=[ap] * len(dsts))],
             local_sem=T.sem.sent)
         sent[0] += n
 
+    def rot(lst, n):
+        n %= len(lst)
+        return lst[n:] + lst[:n]
+
     ranks = [8 * c + j for j in (4, 5, 6, 7)]
     b0 = 256 * c
+    far = [q2, p2, q1, p1]
 
     if k >= 4:
         r = T.rank_of(core)
+        j = k - 4
         g.dma_start(G[:, 64 * r:64 * r + 64], T.x[:, :]).then_inc(T.sem.ld, 16)
         g.wait_ge(T.sem.ld, 16)
-        helpers = [8 * c + 0, 8 * c + 2] + ([8 * c + 3] if k >= 6 else [])
-        send(64 * r, 64 * r + 64, [d for d in ranks if d != core] + helpers, c)
+        order = [4, 0, 6, 2, 7] + ([3] if k >= 6 else []) + [5]
+        send(64 * r, 64 * r + 64, [8 * c + d for d in rot(order, j) if d != k], csem[c])
         g.wait_ge(csem[c], 48)
         if k == 4:
-            send(b0, b0 + 256, [8 * p1 + 1], c)
+            send(b0, b0 + 256, [8 * p1 + 1], csem[c])
         elif k == 6:
-            send(b0, b0 + 256, [8 * q1 + 0], c)
+            send(b0, b0 + 256, [8 * q1 + 0], csem[c])
         elif k == 7:
-            send(b0, b0 + 128, [8 * m + 1], c)
+            send(b0, b0 + 128, [8 * m + 5], T.sem.ml)
         nst = 0
-        for s in (c, m, p2, p1, q2, q1):
-            if s == m:
-                g.wait_ge(csem[s], 32)
-            elif s != c:
-                g.wait_ge(csem[s], 16)
+
+        def store(s):
             g.dma_start(T.y[:, 256 * s:256 * s + 256], G[:, 256 * s:256 * s + 256]).then_inc(T.sem.st, 16)
-            nst += 16
-        g.wait_ge(T.sem.st, nst)
+
+        store(c)
+        if k in (5, 7):
+            g.wait_ge(T.sem.ml, 8)
+            lo = 256 * m + (0 if k == 5 else 128)
+            send(lo, lo + 128, rot([d for d in ranks if d != core], j), csem[m])
+            g.wait_ge(csem[m], 16)
+        else:
+            g.wait_ge(csem[m], 32)
+        store(m)
+        for i in range(4):
+            s = far[(j - i) % 4]
+            g.wait_ge(csem[s], 16)
+            store(s)
+        g.wait_ge(T.sem.st, 16 * 6)
         g.wait_ge(T.sem.sent, sent[0])
         return
 
     if k == 0:
         g.wait_ge(csem[c], 64)
-        send(b0, b0 + 256, [8 * p2 + 3], c)
-        src = [(q2, 0, 256)]
+        send(b0, b0 + 256, [8 * p2 + 3], csem[c])
     elif k == 2:
         g.wait_ge(csem[c], 64)
-        send(b0, b0 + 256, [8 * q2 + 2], c)
-        src = [(q1, 0, 256)]
+        send(b0, b0 + 256, [8 * q2 + 2], csem[c])
     elif k == 3:
         g.wait_ge(csem[c], 32)
-        send(b0 + 128, b0 + 256, [8 * m + 3], c)
-        src = [(m, 128, 256), (p1, 0, 256)]
-    else:
-        src = [(m, 0, 128), (p2, 0, 256)]
-    for s, lo, hi in src:
-        g.wait_ge(csem[s], 8)
-        send(256 * s + lo, 256 * s + hi, ranks, s)
+        send(b0 + 128, b0 + 256, [8 * m + 7], T.sem.ml)
+    s = far[k]
+    g.wait_ge(csem[s], 8)
+    send(256 * s, 256 * s + 256, rot(ranks, k), csem[s])
     g.wait_ge(T.sem.sent, sent[0])

@@ -47,12 +47,11 @@ def rank_program(g, core, T, topo):
             send(b0, b0 + 256, [8 * q1 + 0], csem[c])
         elif k == 7:
             send(b0, b0 + 128, [8 * m + 5], T.sem.ml)
-        nst = 0
 
-        def store(s):
-            g.dma_start(T.y[:, 256 * s:256 * s + 256], G[:, 256 * s:256 * s + 256]).then_inc(T.sem.st, 16)
+        def store_pair(s):
+            lo = 512 * (s // 2)
+            g.dma_start(T.y[:, lo:lo + 512], G[:, lo:lo + 512]).then_inc(T.sem.st, 16)
 
-        store(c)
         if k in (5, 7):
             g.wait_ge(T.sem.ml, 8)
             lo = 256 * m + (0 if k == 5 else 128)
@@ -60,12 +59,12 @@ def rank_program(g, core, T, topo):
             g.wait_ge(csem[m], 16)
         else:
             g.wait_ge(csem[m], 32)
-        store(m)
-        for i in range(4):
-            s = far[(j - i) % 4]
-            g.wait_ge(csem[s], 16)
-            store(s)
-        g.wait_ge(T.sem.st, 16 * 6)
+        store_pair(c)
+        for i in (0, 2):
+            g.wait_ge(csem[far[j ^ i]], 16)
+            g.wait_ge(csem[far[j ^ i ^ 1]], 16)
+            store_pair(far[j ^ i])
+        g.wait_ge(T.sem.st, 16 * 3)
         g.wait_ge(T.sem.sent, sent[0])
         return
 
@@ -80,5 +79,5 @@ def rank_program(g, core, T, topo):
         send(b0 + 128, b0 + 256, [8 * m + 7], T.sem.ml)
     s = far[k]
     g.wait_ge(csem[s], 8)
-    send(256 * s, 256 * s + 256, rot(ranks, k), csem[s])
+    send(256 * s, 256 * s + 256, [ranks[i ^ k] for i in range(4)], csem[s])
     g.wait_ge(T.sem.sent, sent[0])

@@ -5,6 +5,13 @@ SCRATCH = {
 }
 SEMAPHORES = ["ld", "st", "sent", "ml", "c0", "c1", "c2", "c3", "c4", "c5"]
 
+GATHER = {
+    4: [0, 6, 2, 5, 7],
+    5: [4, 0, 6, 2, 7],
+    6: [2, 4, 0, 3, 7, 5],
+    7: [6, 2, 4, 0, 3, 5],
+}
+
 
 def rank_program(g, core, T, topo):
     c, k = divmod(core, 8)
@@ -25,10 +32,6 @@ def rank_program(g, core, T, topo):
             local_sem=T.sem.sent)
         sent[0] += n
 
-    def rot(lst, n):
-        n %= len(lst)
-        return lst[n:] + lst[:n]
-
     ranks = [8 * c + j for j in (4, 5, 6, 7)]
     b0 = 256 * c
     far = [q2, p2, q1, p1]
@@ -38,8 +41,7 @@ def rank_program(g, core, T, topo):
         j = k - 4
         g.dma_start(G[:, 64 * r:64 * r + 64], T.x[:, :]).then_inc(T.sem.ld, 16)
         g.wait_ge(T.sem.ld, 16)
-        order = [4, 0, 6, 2, 7] + ([3] if k >= 6 else []) + [5]
-        send(64 * r, 64 * r + 64, [8 * c + d for d in rot(order, j) if d != k], csem[c])
+        send(64 * r, 64 * r + 64, [8 * c + d for d in GATHER[k]], csem[c])
         g.wait_ge(csem[c], 48)
         if k == 4:
             send(b0, b0 + 256, [8 * p1 + 1], csem[c])
@@ -48,23 +50,25 @@ def rank_program(g, core, T, topo):
         elif k == 7:
             send(b0, b0 + 128, [8 * m + 5], T.sem.ml)
 
-        def store_pair(s):
-            lo = 512 * (s // 2)
-            g.dma_start(T.y[:, lo:lo + 512], G[:, lo:lo + 512]).then_inc(T.sem.st, 16)
+        def store(lo, hi):
+            g.dma_start(T.y[:, lo:hi], G[:, lo:hi]).then_inc(T.sem.st, 16)
 
+        store(b0, b0 + 256)
         if k in (5, 7):
             g.wait_ge(T.sem.ml, 8)
             lo = 256 * m + (0 if k == 5 else 128)
-            send(lo, lo + 128, rot([d for d in ranks if d != core], j), csem[m])
+            others = [4, 6, 7] if k == 5 else [6, 5, 4]
+            send(lo, lo + 128, [8 * c + d for d in others], csem[m])
             g.wait_ge(csem[m], 16)
         else:
             g.wait_ge(csem[m], 32)
-        store_pair(c)
+        store(256 * m, 256 * m + 256)
         for i in (0, 2):
             g.wait_ge(csem[far[j ^ i]], 16)
             g.wait_ge(csem[far[j ^ i ^ 1]], 16)
-            store_pair(far[j ^ i])
-        g.wait_ge(T.sem.st, 16 * 3)
+            lo = 512 * (far[j ^ i] // 2)
+            store(lo, lo + 512)
+        g.wait_ge(T.sem.st, 16 * 4)
         g.wait_ge(T.sem.sent, sent[0])
         return
 

import concourse.bass as bass

SCRATCH = {
    "G": ("sbuf", [128, 1536], "float32"),
}
SEMAPHORES = ["ld", "st", "sent", "ml", "c0", "c1", "c2", "c3", "c4", "c5"]

GATHER = {
    4: [0, 6, 2, 5, 7],
    5: [4, 0, 6, 2, 7],
    6: [2, 4, 0, 3, 7, 5],
    7: [6, 2, 4, 0, 3, 5],
}


def rank_program(g, core, T, topo):
    c, k = divmod(core, 8)
    G = T.G
    csem = [T.sem.c0, T.sem.c1, T.sem.c2, T.sem.c3, T.sem.c4, T.sem.c5]
    m, p1, p2 = c ^ 1, (c + 2) % 6, (c + 4) % 6
    q1, q2 = p1 ^ 1, p2 ^ 1
    sent = [0]

    def send(lo, hi, dsts, sem):
        off = any(topo.chip(d) != c for d in dsts)
        mask, n = (0x00FF, 8) if off else (0xFFFF, 16)
        ap = G[:, lo:hi]
        ids = [bass.DstId(rid=topo.addr(d)[0], pnc=topo.addr(d)[1]) for d in dsts]
        g.remote_dma_fused(
            [bass.RemoteDMATransfer(dst_ids=ids, dma_engine_mask=mask, remote_sem=sem,
                                    srcs=[ap], dsts=[ap] * len(dsts))],
            local_sem=T.sem.sent)
        sent[0] += n

    ranks = [8 * c + j for j in (4, 5, 6, 7)]
    b0 = 256 * c
    far = [q2, p2, q1, p1]

    if k >= 4:
        r = T.rank_of(core)
        j = k - 4
        g.dma_start(G[:, 64 * r:64 * r + 64], T.x[:, :]).then_inc(T.sem.ld, 16)
        g.wait_ge(T.sem.ld, 16)
        send(64 * r, 64 * r + 64, [8 * c + d for d in GATHER[k]], csem[c])
        g.wait_ge(csem[c], 48)
        if k == 4:
            send(b0, b0 + 256, [8 * p1 + 1], csem[c])
        elif k == 6:
            send(b0, b0 + 256, [8 * q1 + 0], csem[c])
        elif k == 7:
            send(b0, b0 + 128, [8 * m + 5], T.sem.ml)

        def store(lo, hi):
            g.dma_start(T.y[:, lo:hi], G[:, lo:hi]).then_inc(T.sem.st, 16)

        store(b0, b0 + 256)
        if k in (5, 7):
            g.wait_ge(T.sem.ml, 8)
            lo = 256 * m + (0 if k == 5 else 128)
            others = [4, 6, 7] if k == 5 else [6, 5, 4]
            send(lo, lo + 128, [8 * c + d for d in others], csem[m])
            g.wait_ge(csem[m], 16)
        else:
            g.wait_ge(csem[m], 32)
        store(256 * m, 256 * m + 256)
        for i in (0, 2):
            g.wait_ge(csem[far[j ^ i]], 16)
            g.wait_ge(csem[far[j ^ i ^ 1]], 16)
            lo = 512 * (far[j ^ i] // 2)
            store(lo, lo + 512)
        g.wait_ge(T.sem.st, 16 * 4)
        g.wait_ge(T.sem.sent, sent[0])
        return

    if k == 0:
        g.wait_ge(csem[c], 64)
        send(b0, b0 + 256, [8 * p2 + 3], csem[c])
    elif k == 2:
        g.wait_ge(csem[c], 64)
        send(b0, b0 + 256, [8 * q2 + 2], csem[c])
    elif k == 3:
        g.wait_ge(csem[c], 32)
        send(b0 + 128, b0 + 256, [8 * m + 7], T.sem.ml)
    s = far[k]
    g.wait_ge(csem[s], 8)
    send(256 * s, 256 * s + 256, [ranks[i ^ k] for i in range(4)], csem[s])
    g.wait_ge(T.sem.sent, sent[0])
